import numpy as np
import ml_dtypes


def mxq(x, axis, fmt="e4m3"):
    dtype, down = {"e4m3": (ml_dtypes.float8_e4m3fn, 7), "e5m2": (ml_dtypes.float8_e5m2, 14)}[fmt]
    v = np.moveaxis(np.asarray(x, np.float32).astype(ml_dtypes.bfloat16).astype(np.float64), axis, -1)
    blocks = v.reshape(v.shape[:-1] + (-1, 32))
    amax = np.abs(blocks).max(-1, keepdims=True)
    byte = np.maximum(np.where(amax > 0, np.frexp(amax)[1] - 1 + 127, 0) - down, 1)
    scale = np.exp2(byte - 127.0)
    codes = (blocks / scale).astype(np.float32).astype(dtype).astype(np.float64)
    return np.moveaxis((codes * scale).reshape(v.shape), -1, axis)


WIDE = False


def mx_kscale(k):
    if not WIDE:
        return np.ones(k)
    levels = np.array([10, -10, 5, -5, 0])
    if k % 512:
        return np.exp2(np.random.permutation(np.resize(levels, k // 32))).repeat(32)
    a = np.empty((k // 512, 16))
    for p in range(k // 512):
        a[p, :8] = np.random.permutation(np.resize(levels, 8))
        for g in range(8):
            far = levels[np.abs(levels - a[p, g]) >= 10]
            a[p, g + 8] = far[np.random.randint(len(far))]
    return np.exp2(a.ravel()).repeat(32)


def f64(x):
    return np.asarray(x).astype(np.float64)


def striped(idx):
    return np.tile(np.asarray(idx).reshape(-1, 16).T, (8, 1)).astype(np.uint16)


def unstriped(offs):
    return offs[:16].T.reshape(-1).astype(np.int64)


E2M1 = np.array([0.0, 0.5, 1.0, 1.5, 2.0, 3.0, 4.0, 6.0, -0.0, -0.5, -1.0, -1.5, -2.0, -3.0, -4.0, -6.0])


def pack_weight(w, fmt):
    k, n = w.shape
    w = f64(np.asarray(w, np.float32).astype(ml_dtypes.bfloat16)).reshape(k // 32, 32, n)
    amax = np.abs(w).max(1)
    if fmt == "e4m3":
        byte = np.frexp(amax)[1] - 1 + 127 - 7
    else:
        mant, ex = np.frexp(amax / 6.0)
        byte = np.where(mant > 0.5, ex, ex - 1) + 127
    byte = np.clip(np.where(amax > 0, byte, 1), 1, 254)
    scaled = (w * np.exp2(127.0 - byte)[:, None, :]).reshape(k, n).astype(np.float32)
    by_word = np.ascontiguousarray(scaled.reshape(k // 512, 128, 4, n).transpose(0, 1, 3, 2))
    if fmt == "e4m3":
        words = by_word.astype(ml_dtypes.float8_e4m3fn).view(np.uint8)
    else:
        c = by_word.astype(ml_dtypes.float4_e2m1fn).view(np.uint8) & 0xF
        words = (c[..., 0::2] | (c[..., 1::2] << 4)).reshape(k // 512, 128, 2 * n)
    return np.ascontiguousarray(words), np.ascontiguousarray(byte.astype(np.uint8).reshape(k // 512, 16, n))


def unpack_weight(words, scales, fmt):
    g, _, n = scales.shape
    words = np.ascontiguousarray(words).reshape(g, 128, n, -1)
    if fmt == "e4m3":
        vals = words.view(ml_dtypes.float8_e4m3fn).astype(np.float64)
    else:
        nib = np.empty((g, 128, n, 4), np.uint8)
        nib[..., 0::2] = words & 0xF
        nib[..., 1::2] = words >> 4
        vals = E2M1[nib]
    vals = vals * np.repeat(np.exp2(scales.astype(np.float64) - 127.0), 8, axis=1)[..., None]
    return vals.transpose(0, 1, 3, 2).reshape(g * 512, n)


D, T, U, I, J, G = 512, 1024, 1024, 256, 512, 64


def setup_inputs():
    n = np.random.standard_normal
    idx = np.random.permutation(T)[:I]
    idx2 = np.random.permutation(U)[:J]
    fd = mx_kscale(D)
    fj = mx_kscale(J)
    tj = np.ones(U)
    tj[idx2] = fj
    tabbp = pack_weight(n((D, U)) / fd[:, None], "e2m1")
    return {
        "taba": (n((D, T)) * 1 / np.sqrt(D) * fd[:, None]).astype(np.float32),
        "tabb_words": tabbp[0],
        "tabb_scales": tabbp[1],
        "gw": (np.random.uniform(0.5, 2.0, (I, G))).astype(np.float32),
        "js": (np.random.uniform(2.0, 8.0, (1, J)) * fj).astype(np.float32),
        "brows": (n((D, U)) / tj).astype(np.float32),
        "old": (n((D, T)) * 2.0).astype(np.float32),
        "fade": (np.random.uniform(0.5, 1.0, (1, T))).astype(np.float32),
        "offs": striped(idx),
        "offs2": striped(idx2),
    }


def reference(taba, tabb_words, tabb_scales, gw, js, brows, old, fade, offs, offs2):
    idx = unstriped(offs)
    idx2 = unstriped(offs2)
    tabbu = unpack_weight(tabb_words, tabb_scales, "e2m1")
    tabaidxq = mxq(f64(taba)[:, idx], 0, "e4m3")
    tabbidx2g = tabbu[:, idx2]
    s = tabaidxq.T @ tabbidx2g
    b = s - np.max(s, axis=1, keepdims=True)
    p = np.exp(b)
    z = np.sum(p, axis=1, keepdims=True)
    s1g = p.reshape(I, G, J // G).sum(axis=2)
    ds1g = f64(gw) / (s1g / z + 0.002) / z
    r1 = np.repeat(ds1g, J // G, axis=1)
    dz = np.sum(f64(gw) / (s1g / z + 0.002) * s1g / np.square(z) * (-1.0), axis=1, keepdims=True)
    dp = r1 + dz
    db = dp * p
    gs = db * f64(js)
    gt1 = gs.T
    bt = f64(brows)[:, idx2].T
    btq = mxq(bt, 0, "e4m3")
    gt1q = mxq(gt1, 0, "e4m3")
    gx1 = btq.T @ gt1q
    gf = np.zeros((D, T))
    gf[:, idx] = gx1
    y = f64(old) * f64(fade) + gf
    return y

@@ -1,0 +1,226 @@
+from contextlib import ExitStack
+
+import concourse.mybir as mybir
+from concourse.masks import make_identity
+
+D, T, U, I, J, G = 512, 1024, 1024, 256, 512, 64
+FLOPS = 2 * D * I * J + 2 * J * D * I
+
+F32 = mybir.dt.float32
+BF16 = mybir.dt.bfloat16
+I32 = mybir.dt.int32
+U32 = mybir.dt.uint32
+U16 = mybir.dt.uint16
+U8 = mybir.dt.uint8
+FP8X4 = mybir.dt.float8_e4m3fn_x4
+FP4X4 = mybir.dt.float4_e2m1fn_x4
+ALU = mybir.AluOpType
+ACT = mybir.ActivationFunctionType
+AXIS_X = mybir.AxisListType.X
+
+P = 128
+PACK = 4
+BANK = 512
+GROUP = J // G
+EPS = 0.002
+
+
+def tile_attend_bgrouplogshare_x_kernel(tc, taba, tabb_words, tabb_scales, gw, js, brows, old, fade, offs, offs2, out):
+    nc = tc.nc
+    with ExitStack() as ctx:
+        keep = ctx.enter_context(tc.tile_pool(name="keep", bufs=1))
+        psum = ctx.enter_context(tc.psum_pool(name="psum", bufs=1))
+
+        def sb(name, shape, dtype, on=None):
+            return keep.tile(shape, dtype, name=name, tag=on or name, align_bytes=64)
+
+        def bank(name, number):
+            return psum.tile([P, BANK], F32, name=name, tag="bank%d" % number)
+
+        first_list = keep.tile([P, I // 16], U16, name="first_list")
+        second_list = keep.tile([P, J // 16], U16, name="second_list")
+
+        scale_table = sb("scale_table", [P, U], U8)
+        nc.gpsimd.memset(scale_table[:].bitcast(I32), 0)
+        nc.sync.dma_start(second_list[:], offs2)
+        word_table = sb("word_table", [P, U], U16)
+        nc.sync.dma_start(word_table[:].bitcast(I32), tabb_words[0].bitcast(I32))
+        for q in range(4):
+            nc.sync.dma_start(
+                scale_table[32 * q : 32 * q + 4, :].bitcast(I32), tabb_scales[0, 4 * q : 4 * q + 4, :].bitcast(I32)
+            )
+        ident = sb("ident", [P, P], F32)
+        vec_rows = sb("vec_rows", [P, P], F32)
+        nc.gpsimd.memset(vec_rows[:], 0.0)
+        make_identity(nc, ident[:])
+        taba_rows = taba.rearrange("(p t) c -> p t c", t=PACK)
+        a_first = sb("a_first", [P, 2, T], F32)
+        a_planes = [a_first[:, 0, :], a_first[:, 1, :]]
+        nc.sync.dma_start(a_first[:], taba_rows[:, 0:2, :])
+        nc.sync.dma_start(first_list[:], offs)
+        nc.sync.dma_start(vec_rows[8:12, :], js.rearrange("o (b p) -> (o b) p", p=P))
+        nc.sync.dma_start(vec_rows[0:8, :], fade.rearrange("o (b p) -> (o b) p", p=P))
+        for t in range(2, PACK):
+            a_plane = sb("a_plane%d" % t, [P, T], F32)
+            nc.sync.dma_start(a_plane[:], taba_rows[:, t, :])
+            a_planes.append(a_plane[:])
+        weights = sb("weights", [P, 2, G], F32)
+        nc.sync.dma_start(weights[:], gw.rearrange("(a p) g -> p a g", p=P))
+
+        brows_rows = brows.rearrange("(m p) c -> p m c", p=P)
+        old_rows = old.rearrange("(m p) c -> p m c", p=P)
+        b_raw = {}
+        for k in range(2):
+            for h in range(2):
+                b_raw[k, h] = sb("b_raw%d%d" % (k, h), [P, 2, BANK], F32)
+                nc.sync.dma_start(b_raw[k, h][:], brows_rows[:, 2 * k : 2 * k + 2, h * BANK : (h + 1) * BANK])
+        turned_planes = 4
+        old_half = [sb("old_half%d" % h, [P, turned_planes, BANK], F32) for h in range(2)]
+        for h in range(2):
+            nc.sync.dma_start(old_half[h][:], old_rows[:, 0:turned_planes, h * BANK : (h + 1) * BANK])
+
+        windows = [sb("window%d" % m, [P, T], F32) for m in range(4)]
+        for m in range(4):
+            (nc.vector if m < 3 else nc.gpsimd).memset(windows[m][:], 0.0)
+
+        vec_turned = bank("vec_turned", 5)
+        nc.tensor.transpose(vec_turned[:, 0:P], vec_rows[:], ident[:])
+        vec_cols = sb("vec_cols", [P, 16], F32)
+        nc.scalar.activation(vec_cols[:], vec_turned[:, 0:16], ACT.Copy)
+        js_spread = bank("js_spread", 4)
+        for c in range(4):
+            nc.tensor.transpose(js_spread[:, c * P : (c + 1) * P], vec_cols[:, 8 + c : 9 + c].to_broadcast([P, P]), ident[:])
+
+        b_words = sb("b_words", [P, J], U16)
+        nc.vector.tensor_copy(b_words[:], word_table[:].indirect(second_list[:]))
+        b_scales = sb("b_scales", [P, J], U8)
+        nc.vector.tensor_copy(b_scales[:], scale_table[:].indirect(second_list[:]))
+        a_woven = sb("a_woven", [P, I, PACK], BF16)
+        for t in range(PACK):
+            nc.vector.tensor_copy(a_woven[:, :, t], a_planes[t].indirect(first_list[:]))
+        a_codes = sb("a_codes", [P, I], U32)
+        a_scales = sb("a_scales", [P, I], U8)
+        nc.vector.quantize_mx(a_codes[:].bitcast(FP8X4), a_scales[:], a_woven[:].rearrange("p i t -> p (i t)"))
+
+        scores = [bank("scores%d" % a, a) for a in range(2)]
+        for a in range(2):
+            cols = slice(a * P, (a + 1) * P)
+            nc.tensor.matmul_mx(
+                scores[a][:], lhsT=a_codes[:, cols].bitcast(FP8X4), lhsT_scale=a_scales[:, cols],
+                rhs=b_words[:].bitcast(FP4X4), rhs_scale=b_scales[:], start=True, stop=True,
+            )
+
+        b_pairs = [sb("b_pairs%d" % k, [P, U, 2], BF16) for k in range(2)]
+
+        def cast_pairs(k):
+            for h in range(2):
+                nc.scalar.activation(
+                    b_pairs[k][:, h * BANK : (h + 1) * BANK, :], b_raw[k, h][:].rearrange("p e c -> p c e"), ACT.Copy
+                )
+
+        r_codes = sb("r_codes", [P, D], U32)
+        r_scales = sb("r_scales", [P, D], U8)
+        r_woven = [sb("r_woven%d" % k, [P, 2, P, PACK], BF16) for k in range(2)]
+
+        def pick_rows(k):
+            picked = sb("picked%d" % k, [P, PACK, P], U32)
+            nc.vector.tensor_copy(
+                picked[:].rearrange("p t s -> p s t"),
+                b_pairs[k][:].rearrange("p c e -> p (c e)").bitcast(U32).indirect(second_list[:]),
+            )
+            r_turned = bank("r_turned%d" % k, 2 + k)
+            for t in range(PACK):
+                nc.tensor.transpose(r_turned[:, t * P : (t + 1) * P], picked[:, t, :].bitcast(F32), ident[:])
+            nc.scalar.copy(r_woven[k][:], r_turned[:].bitcast(BF16).rearrange("p (t d e) -> p e d t", t=PACK, e=2))
+
+        def quantise_rows(k):
+            cols = slice(2 * k * P, (2 * k + 2) * P)
+            nc.vector.quantize_mx(r_codes[:, cols].bitcast(FP8X4), r_scales[:, cols], r_woven[k][:].rearrange("p e d t -> p (e d t)"))
+
+        cast_pairs(0)
+
+        st = {}
+        for a in range(2):
+            for name, width in (("nmax", 1), ("z", 1), ("rz", 1), ("pos", 1), ("s1g", G), ("share", G), ("inv", G), ("ds", G), ("junk", G), ("pj", J)):
+                st[name, a] = sb("%s%d" % (name, a), [P, width], F32)
+            st["p", a] = sb("p%d" % a, [P, J], F32, on="b_raw01" if a == 0 else None)
+            st["gs", a] = sb("gs%d" % a, [P, J], BF16)
+            st["woven", a] = sb("g_woven%d" % a, [P, J], BF16)
+        g_codes = sb("g_codes", [P, I], U32)
+        g_scales = sb("g_scales", [P, I], U8)
+
+        for a in range(2):
+            nc.vector.tensor_reduce(st["nmax", a][:], scores[a][:], AXIS_X, ALU.max, negate=True)
+            nc.scalar.activation(st["p", a][:], scores[a][:], ACT.Exp, bias=st["nmax", a][:], accum_out=st["z", a][:])
+        cast_pairs(1)
+        pick_rows(0)
+        for a in range(2):
+            nc.vector.tensor_reduce(st["s1g", a][:], st["p", a][:].rearrange("p (g r) -> p g r", r=GROUP), AXIS_X, ALU.add)
+            nc.vector.reciprocal(st["rz", a][:], st["z", a][:])
+        for a in range(2):
+            nc.vector.tensor_scalar(st["share", a][:], st["s1g", a][:], st["rz", a][:], EPS, ALU.mult, ALU.add)
+        for a in range(2):
+            nc.vector.reciprocal(st["inv", a][:], st["share", a][:])
+        for a in range(2):
+            nc.vector.scalar_tensor_tensor(st["ds", a][:], st["inv", a][:], st["rz", a][:], weights[:, a, :], ALU.mult, ALU.mult)
+            nc.vector.tensor_tensor(st["pj", a][:], st["p", a][:], js_spread[:], ALU.mult)
+        for a in range(2):
+            nc.vector.scalar_tensor_tensor(
+                st["junk", a][:], st["ds", a][:], st["rz", a][:], st["s1g", a][:], ALU.mult, ALU.mult, accum_out=st["pos", a][:]
+            )
+        pick_rows(1)
+        for a in range(2):
+            nc.vector.scalar_tensor_tensor(
+                st["gs", a][:].rearrange("p (g r) -> p g r", r=GROUP),
+                st["ds", a][:].unsqueeze(2).to_broadcast([P, G, GROUP]),
+                st["pos", a][:],
+                st["pj", a][:].rearrange("p (g r) -> p g r", r=GROUP),
+                ALU.subtract, ALU.mult,
+            )
+            g_turned = bank("g_turned%d" % a, a)
+            pairs = st["gs", a][:].bitcast(F32)
+            for u in range(2):
+                nc.tensor.transpose(g_turned[:, u * P : (u + 1) * P], pairs[:, u : 2 * P : 2], ident[:])
+            nc.scalar.copy(
+                st["woven", a][:].bitcast(F32).rearrange("p (i u) -> p i u", u=2),
+                g_turned[:, 0 : 2 * P].rearrange("p (u i) -> p i u", u=2),
+            )
+        for k in range(2):
+            quantise_rows(k)
+        for a in range(2):
+            cols = slice(a * P, (a + 1) * P)
+            nc.vector.quantize_mx(g_codes[:, cols].bitcast(FP8X4), g_scales[:, cols], st["woven", a][:])
+
+        order = (0, 1, 2, 3)
+        grads = [sb("grad%d" % m, [P, I], F32) for m in range(4)]
+        for n, m in enumerate(order):
+            cols = slice(m * P, (m + 1) * P)
+            product = bank("product%d" % m, (2, 3, 0, 1)[n])
+            nc.tensor.matmul_mx(
+                product[:, 0:I], lhsT=r_codes[:, cols].bitcast(FP8X4), lhsT_scale=r_scales[:, cols],
+                rhs=g_codes[:].bitcast(FP8X4), rhs_scale=g_scales[:], start=True, stop=True,
+            )
+            nc.scalar.copy(grads[m][:], product[:, 0:I])
+
+        faded = [sb("faded%d" % b, [P, turned_planes, P], F32) for b in range(8)]
+        for b in range(8):
+            h, bb = divmod(b, 4)
+            old_turned = bank("old_turned%d" % b, 5 + b % 3)
+            for m in range(turned_planes):
+                nc.tensor.transpose(old_turned[:, m * P : (m + 1) * P], old_half[h][:, m, bb * P : (bb + 1) * P], ident[:])
+            nc.scalar.activation(
+                faded[b][:].rearrange("p m d -> p (m d)"), old_turned[:, 0 : turned_planes * P], ACT.Copy, scale=vec_cols[:, b : b + 1]
+            )
+
+        out_rows = out.rearrange("(m p) c -> p m c", p=P)
+        for m in order:
+            nc.vector.tensor_copy(windows[m][:].indirect(first_list[:]), grads[m][:])
+            for h in range(2):
+                half = slice(h * BANK, (h + 1) * BANK)
+                result = sb("result%d%d" % (m, h), [P, BANK], F32)
+                if m < turned_planes:
+                    back = bank("back%d%d" % (m, h), (5, 6, 7, 4, 2, 3, 0, 1)[2 * m + h])
+                    for bb in range(4):
+                        nc.tensor.transpose(back[:, bb * P : (bb + 1) * P], faded[4 * h + bb][:, m, :], ident[:])
+                    nc.vector.tensor_tensor(result[:], back[:], windows[m][:, half], ALU.add)
+                nc.sync.dma_start(out_rows[:, m, half], result[:])

@@ -74,22 +74,30 @@ def tile_attend_bgrouplogshare_x_kernel(tc, taba, tabb_words, tabb_scales, gw, j
             for h in range(2):
                 b_raw[k, h] = sb("b_raw%d%d" % (k, h), [P, 2, BANK], F32)
                 nc.sync.dma_start(b_raw[k, h][:], brows_rows[:, 2 * k : 2 * k + 2, h * BANK : (h + 1) * BANK])
-        turned_planes = 4
+        turned_planes = 3
         old_half = [sb("old_half%d" % h, [P, turned_planes, BANK], F32) for h in range(2)]
         for h in range(2):
-            nc.sync.dma_start(old_half[h][:], old_rows[:, 0:turned_planes, h * BANK : (h + 1) * BANK])
+            nc.sync.dma_start(old_half[h][:], old_rows[:, 1:4, h * BANK : (h + 1) * BANK])
+        old_plain = sb("old_plain", [P, T], F32)
+        nc.sync.dma_start(old_plain[:], old_rows[:, 0, :])
 
         windows = [sb("window%d" % m, [P, T], F32) for m in range(4)]
         for m in range(4):
-            (nc.vector if m < 3 else nc.gpsimd).memset(windows[m][:], 0.0)
+            (nc.vector if m < 1 else nc.gpsimd).memset(windows[m][:], 0.0)
 
         vec_turned = bank("vec_turned", 5)
         nc.tensor.transpose(vec_turned[:, 0:P], vec_rows[:], ident[:])
         vec_cols = sb("vec_cols", [P, 16], F32)
         nc.scalar.activation(vec_cols[:], vec_turned[:, 0:16], ACT.Copy)
-        js_spread = bank("js_spread", 4)
-        for c in range(4):
-            nc.tensor.transpose(js_spread[:, c * P : (c + 1) * P], vec_cols[:, 8 + c : 9 + c].to_broadcast([P, P]), ident[:])
+        spread = sb("spread", [P, 3 * BANK], F32)
+        for n in range(3):
+            spread_bank = bank("spread_bank%d" % n, (6, 7, 4)[n])
+            for c in range(4):
+                column = vec_cols[:, 4 * n + c : 4 * n + c + 1]
+                nc.tensor.transpose(spread_bank[:, c * P : (c + 1) * P], column.to_broadcast([P, P]), ident[:])
+            nc.scalar.copy(spread[:, n * BANK : (n + 1) * BANK], spread_bank[:])
+        fade_spread = spread[:, 0:T]
+        js_spread = spread[:, T : T + J]
 
         b_words = sb("b_words", [P, J], U16)
         nc.vector.tensor_copy(b_words[:], word_table[:].indirect(second_list[:]))
@@ -112,115 +120,138 @@ def tile_attend_bgrouplogshare_x_kernel(tc, taba, tabb_words, tabb_scales, gw, j
 
         b_pairs = [sb("b_pairs%d" % k, [P, U, 2], BF16) for k in range(2)]
 
-        def cast_pairs(k):
-            for h in range(2):
-                nc.scalar.activation(
-                    b_pairs[k][:, h * BANK : (h + 1) * BANK, :], b_raw[k, h][:].rearrange("p e c -> p c e"), ACT.Copy
-                )
+        def cast_pairs(k, h):
+            nc.scalar.activation(
+                b_pairs[k][:, h * BANK : (h + 1) * BANK, :], b_raw[k, h][:].rearrange("p e c -> p c e"), ACT.Copy
+            )
 
         r_codes = sb("r_codes", [P, D], U32)
         r_scales = sb("r_scales", [P, D], U8)
         r_woven = [sb("r_woven%d" % k, [P, 2, P, PACK], BF16) for k in range(2)]
 
         def pick_rows(k):
-            picked = sb("picked%d" % k, [P, PACK, P], U32)
-            nc.vector.tensor_copy(
-                picked[:].rearrange("p t s -> p s t"),
-                b_pairs[k][:].rearrange("p c e -> p (c e)").bitcast(U32).indirect(second_list[:]),
-            )
+            picked = sb("picked%d" % k, [P, J], U32)
+            nc.vector.tensor_copy(picked[:], b_pairs[k][:].rearrange("p c e -> p (c e)").bitcast(U32).indirect(second_list[:]))
             r_turned = bank("r_turned%d" % k, 2 + k)
             for t in range(PACK):
-                nc.tensor.transpose(r_turned[:, t * P : (t + 1) * P], picked[:, t, :].bitcast(F32), ident[:])
+                nc.tensor.transpose(r_turned[:, t * P : (t + 1) * P], picked[:].bitcast(F32)[:, t:J:PACK], ident[:])
             nc.scalar.copy(r_woven[k][:], r_turned[:].bitcast(BF16).rearrange("p (t d e) -> p e d t", t=PACK, e=2))
 
         def quantise_rows(k):
             cols = slice(2 * k * P, (2 * k + 2) * P)
             nc.vector.quantize_mx(r_codes[:, cols].bitcast(FP8X4), r_scales[:, cols], r_woven[k][:].rearrange("p e d t -> p (e d t)"))
 
-        cast_pairs(0)
+        cast_pairs(0, 0)
 
-        st = {}
-        for a in range(2):
-            for name, width in (("nmax", 1), ("z", 1), ("rz", 1), ("pos", 1), ("s1g", G), ("share", G), ("inv", G), ("ds", G), ("junk", G), ("pj", J)):
-                st[name, a] = sb("%s%d" % (name, a), [P, width], F32)
-            st["p", a] = sb("p%d" % a, [P, J], F32, on="b_raw01" if a == 0 else None)
-            st["gs", a] = sb("gs%d" % a, [P, J], BF16)
-            st["woven", a] = sb("g_woven%d" % a, [P, J], BF16)
+        neg_max = [sb("neg_max%d" % a, [P, 1], F32) for a in range(2)]
+        total = sb("total", [P, 2], F32)
+        inv_total = sb("inv_total", [P, 2], F32)
+        probs = sb("probs", [P, 2, J], F32, on="b_raw00")
+        scaled = [sb("scaled%d" % a, [P, J], F32) for a in range(2)]
+        group_sum = sb("group_sum", [P, 2, G], F32)
+        denom = sb("denom", [P, 2, G], F32)
+        inv_denom = sb("inv_denom", [P, 2, G], F32)
+        ds = sb("ds", [P, 2, G], F32)
+        terms = [sb("terms%d" % a, [P, G], F32) for a in range(2)]
+        shift = [sb("shift%d" % a, [P, 1], F32) for a in range(2)]
+        gs = [sb("gs%d" % a, [P, J], BF16) for a in range(2)]
+        g_woven = [sb("g_woven%d" % a, [P, P * PACK], BF16) for a in range(2)]
         g_codes = sb("g_codes", [P, I], U32)
         g_scales = sb("g_scales", [P, I], U8)
 
         for a in range(2):
-            nc.vector.tensor_reduce(st["nmax", a][:], scores[a][:], AXIS_X, ALU.max, negate=True)
-            nc.scalar.activation(st["p", a][:], scores[a][:], ACT.Exp, bias=st["nmax", a][:], accum_out=st["z", a][:])
-        cast_pairs(1)
+            nc.vector.tensor_reduce(neg_max[a][:], scores[a][:], AXIS_X, ALU.max, negate=True)
+            nc.scalar.activation(probs[:, a, :], scores[a][:], ACT.Exp, bias=neg_max[a][:], accum_out=total[:, a : a + 1])
+            nc.gpsimd.tensor_tensor(scaled[a][:], probs[:, a, :], js_spread, ALU.mult)
+        cast_pairs(0, 1)
+        cast_pairs(1, 0)
+        cast_pairs(1, 1)
+        for a in range(2):
+            nc.vector.tensor_reduce(group_sum[:, a, :], probs[:, a, :].rearrange("p (g r) -> p g r", r=GROUP), AXIS_X, ALU.add)
+        nc.vector.scalar_tensor_tensor(
+            denom[:], total[:].unsqueeze(2).to_broadcast([P, 2, G]), EPS, group_sum[:], ALU.mult, ALU.add
+        )
+        nc.vector.reciprocal(inv_total[:], total[:])
+        nc.vector.reciprocal(inv_denom[:], denom[:])
         pick_rows(0)
-        for a in range(2):
-            nc.vector.tensor_reduce(st["s1g", a][:], st["p", a][:].rearrange("p (g r) -> p g r", r=GROUP), AXIS_X, ALU.add)
-            nc.vector.reciprocal(st["rz", a][:], st["z", a][:])
-        for a in range(2):
-            nc.vector.tensor_scalar(st["share", a][:], st["s1g", a][:], st["rz", a][:], EPS, ALU.mult, ALU.add)
-        for a in range(2):
-            nc.vector.reciprocal(st["inv", a][:], st["share", a][:])
-        for a in range(2):
-            nc.vector.scalar_tensor_tensor(st["ds", a][:], st["inv", a][:], st["rz", a][:], weights[:, a, :], ALU.mult, ALU.mult)
-            nc.vector.tensor_tensor(st["pj", a][:], st["p", a][:], js_spread[:], ALU.mult)
-        for a in range(2):
-            nc.vector.scalar_tensor_tensor(
-                st["junk", a][:], st["ds", a][:], st["rz", a][:], st["s1g", a][:], ALU.mult, ALU.mult, accum_out=st["pos", a][:]
-            )
         pick_rows(1)
+        nc.vector.tensor_tensor(ds[:], inv_denom[:], weights[:], ALU.mult)
         for a in range(2):
             nc.vector.scalar_tensor_tensor(
-                st["gs", a][:].rearrange("p (g r) -> p g r", r=GROUP),
-                st["ds", a][:].unsqueeze(2).to_broadcast([P, G, GROUP]),
-                st["pos", a][:],
-                st["pj", a][:].rearrange("p (g r) -> p g r", r=GROUP),
+                terms[a][:], ds[:, a, :], inv_total[:, a : a + 1], group_sum[:, a, :], ALU.mult, ALU.mult, accum_out=shift[a][:]
+            )
+        for a in range(2):
+            nc.vector.scalar_tensor_tensor(
+                gs[a][:].rearrange("p (g r) -> p g r", r=GROUP),
+                ds[:, a, :].unsqueeze(2).to_broadcast([P, G, GROUP]),
+                shift[a][:],
+                scaled[a][:].rearrange("p (g r) -> p g r", r=GROUP),
                 ALU.subtract, ALU.mult,
             )
             g_turned = bank("g_turned%d" % a, a)
-            pairs = st["gs", a][:].bitcast(F32)
+            pairs = gs[a][:].bitcast(F32)
             for u in range(2):
                 nc.tensor.transpose(g_turned[:, u * P : (u + 1) * P], pairs[:, u : 2 * P : 2], ident[:])
             nc.scalar.copy(
-                st["woven", a][:].bitcast(F32).rearrange("p (i u) -> p i u", u=2),
+                g_woven[a][:].bitcast(F32).rearrange("p (i u) -> p i u", u=2),
                 g_turned[:, 0 : 2 * P].rearrange("p (u i) -> p i u", u=2),
             )
-        for k in range(2):
-            quantise_rows(k)
+
+        def product(into, m, cols):
+            rows = slice(m * P, (m + 1) * P)
+            nc.tensor.matmul_mx(
+                into, lhsT=r_codes[:, rows].bitcast(FP8X4), lhsT_scale=r_scales[:, rows],
+                rhs=g_codes[:, cols].bitcast(FP8X4), rhs_scale=g_scales[:, cols], start=True, stop=True,
+            )
+
+        quantise_rows(0)
+        early = [sb("early%d" % a, [P, 2, P], F32) for a in range(2)]
         for a in range(2):
             cols = slice(a * P, (a + 1) * P)
-            nc.vector.quantize_mx(g_codes[:, cols].bitcast(FP8X4), g_scales[:, cols], st["woven", a][:])
-
-        order = (0, 1, 2, 3)
-        grads = [sb("grad%d" % m, [P, I], F32) for m in range(4)]
-        for n, m in enumerate(order):
-            cols = slice(m * P, (m + 1) * P)
-            product = bank("product%d" % m, (2, 3, 0, 1)[n])
-            nc.tensor.matmul_mx(
-                product[:, 0:I], lhsT=r_codes[:, cols].bitcast(FP8X4), lhsT_scale=r_scales[:, cols],
-                rhs=g_codes[:].bitcast(FP8X4), rhs_scale=g_scales[:], start=True, stop=True,
-            )
-            nc.scalar.copy(grads[m][:], product[:, 0:I])
+            nc.vector.quantize_mx(g_codes[:, cols].bitcast(FP8X4), g_scales[:, cols], g_woven[a][:])
+            early_bank = bank("early_bank%d" % a, (2, 0)[a])
+            for m in range(2):
+                product(early_bank[:, m * P : (m + 1) * P], m, cols)
+            nc.scalar.copy(early[a][:].rearrange("p m i -> p (m i)"), early_bank[:, 0 : 2 * P])
+        faded_first = sb("faded_first", [P, T], F32, on="g_woven1")
+        nc.gpsimd.tensor_tensor(faded_first[:], old_plain[:], fade_spread, ALU.mult)
+        quantise_rows(1)
+        late = {m: sb("late%d" % m, [P, I], F32) for m in (2, 3)}
+        for m in (2, 3):
+            late_bank = bank("late_bank%d" % m, (1, 3)[m - 2])
+            product(late_bank[:, 0:I], m, slice(0, I))
+            nc.scalar.copy(late[m][:], late_bank[:, 0:I])
 
         faded = [sb("faded%d" % b, [P, turned_planes, P], F32) for b in range(8)]
         for b in range(8):
             h, bb = divmod(b, 4)
-            old_turned = bank("old_turned%d" % b, 5 + b % 3)
-            for m in range(turned_planes):
-                nc.tensor.transpose(old_turned[:, m * P : (m + 1) * P], old_half[h][:, m, bb * P : (bb + 1) * P], ident[:])
+            old_turned = bank("old_turned%d" % b, 4 + b % 4)
+            for n in range(turned_planes):
+                nc.tensor.transpose(old_turned[:, n * P : (n + 1) * P], old_half[h][:, n, bb * P : (bb + 1) * P], ident[:])
             nc.scalar.activation(
                 faded[b][:].rearrange("p m d -> p (m d)"), old_turned[:, 0 : turned_planes * P], ACT.Copy, scale=vec_cols[:, b : b + 1]
             )
 
         out_rows = out.rearrange("(m p) c -> p m c", p=P)
-        for m in order:
-            nc.vector.tensor_copy(windows[m][:].indirect(first_list[:]), grads[m][:])
-            for h in range(2):
-                half = slice(h * BANK, (h + 1) * BANK)
-                result = sb("result%d%d" % (m, h), [P, BANK], F32)
-                if m < turned_planes:
-                    back = bank("back%d%d" % (m, h), (5, 6, 7, 4, 2, 3, 0, 1)[2 * m + h])
-                    for bb in range(4):
-                        nc.tensor.transpose(back[:, bb * P : (bb + 1) * P], faded[4 * h + bb][:, m, :], ident[:])
+        for a in range(2):
+            for m in range(2):
+                nc.vector.tensor_copy(windows[m][:].indirect(first_list[:, 8 * a : 8 * a + 8]), early[a][:, m, :])
+        for m in (2, 3):
+            nc.vector.tensor_copy(windows[m][:].indirect(first_list[:]), late[m][:])
+        for n in range(8):
+            m, h = divmod(n, 2)
+            half = slice(h * BANK, (h + 1) * BANK)
+            result = sb("result%d" % n, [P, BANK], F32)
+            if m == 0:
+                nc.gpsimd.tensor_tensor(result[:], faded_first[:, half], windows[m][:, half], ALU.add)
+            else:
+                back = bank("back%d" % n, (4, 5, 6, 4, 5, 6)[n - 2])
+                for bb in range(4):
+                    nc.tensor.transpose(back[:, bb * P : (bb + 1) * P], faded[4 * h + bb][:, m - 1, :], ident[:])
+                if n < 4:
+                    faded_back = sb("faded_back%d" % n, [P, BANK], F32)
+                    nc.scalar.copy(faded_back[:], back[:])
+                    nc.gpsimd.tensor_tensor(result[:], faded_back[:], windows[m][:, half], ALU.add)
+                else:
                     nc.vector.tensor_tensor(result[:], back[:], windows[m][:, half], ALU.add)
-                nc.sync.dma_start(out_rows[:, m, half], result[:])
+            (nc.sync if n < 4 else nc.scalar).dma_start(out_rows[:, m, half], result[:])

@@ -69,17 +69,19 @@ def tile_attend_bgrouplogshare_x_kernel(tc, taba, tabb_words, tabb_scales, gw, j
 
         brows_rows = brows.rearrange("(m p) c -> p m c", p=P)
         old_rows = old.rearrange("(m p) c -> p m c", p=P)
-        b_raw = {}
-        for k in range(2):
-            for h in range(2):
-                b_raw[k, h] = sb("b_raw%d%d" % (k, h), [P, 2, BANK], F32)
-                nc.sync.dma_start(b_raw[k, h][:], brows_rows[:, 2 * k : 2 * k + 2, h * BANK : (h + 1) * BANK])
-        turned_planes = 3
+        old_plain = [sb("old_plain%d" % m, [P, T], F32) for m in range(2)]
+        b_planes = [sb("b_plane%d" % m, [P, U], F32) for m in range(2)]
+        nc.sync.dma_start(b_planes[0][:], brows_rows[:, 0, :])
+        nc.sync.dma_start(old_plain[0][:], old_rows[:, 0, :])
+        nc.sync.dma_start(b_planes[1][:], brows_rows[:, 1, :])
+        b_raw = [sb("b_raw%d" % h, [P, 2, BANK], F32) for h in range(2)]
+        for h in range(2):
+            nc.sync.dma_start(b_raw[h][:], brows_rows[:, 2:4, h * BANK : (h + 1) * BANK])
+        turned_planes = 2
         old_half = [sb("old_half%d" % h, [P, turned_planes, BANK], F32) for h in range(2)]
         for h in range(2):
-            nc.sync.dma_start(old_half[h][:], old_rows[:, 1:4, h * BANK : (h + 1) * BANK])
-        old_plain = sb("old_plain", [P, T], F32)
-        nc.sync.dma_start(old_plain[:], old_rows[:, 0, :])
+            nc.sync.dma_start(old_half[h][:], old_rows[:, 2:4, h * BANK : (h + 1) * BANK])
+        nc.sync.dma_start(old_plain[1][:], old_rows[:, 1, :])
 
         windows = [sb("window%d" % m, [P, T], F32) for m in range(4)]
         for m in range(4):
@@ -118,78 +120,104 @@ def tile_attend_bgrouplogshare_x_kernel(tc, taba, tabb_words, tabb_scales, gw, j
                 rhs=b_words[:].bitcast(FP4X4), rhs_scale=b_scales[:], start=True, stop=True,
             )
 
-        b_pairs = [sb("b_pairs%d" % k, [P, U, 2], BF16) for k in range(2)]
+        r_codes, r_scales = {}, {}
+        r_woven = [sb("r_woven%d" % k, [P, 2, P, PACK], BF16) for k in range(2)]
+        picked = {}
 
-        def cast_pairs(k, h):
-            nc.scalar.activation(
-                b_pairs[k][:, h * BANK : (h + 1) * BANK, :], b_raw[k, h][:].rearrange("p e c -> p c e"), ACT.Copy
+        def pick_on_vector(m, on=None):
+            picked[m] = sb("picked%d" % m, [P, J], BF16, on=on)
+            nc.vector.tensor_copy(picked[m][:], b_planes[m][:].indirect(second_list[:]))
+
+        def pick_on_scalar(m, on=None, on2=None):
+            rounded = sb("rounded%d" % m, [P, U], BF16, on=on)
+            nc.scalar.activation(rounded[:], b_planes[m][:], ACT.Copy)
+            picked[m] = sb("picked%d" % m, [P, J], BF16, on=on2)
+            for h in range(1):
+                n = J // 1
+                nc.scalar.activation(picked[m][:, h * n : (h + 1) * n], rounded[:].indirect(second_list[:, h * n // 16 : (h + 1) * n // 16]), ACT.Copy)
+
+        b_pairs = sb("b_pairs", [P, U, 2], BF16)
+
+        def cast_pairs():
+            for h in range(2):
+                nc.scalar.activation(b_pairs[:, h * BANK : (h + 1) * BANK, :], b_raw[h][:].rearrange("p e c -> p c e"), ACT.Copy)
+
+        def pick_pairs(on=None):
+            picked[2] = sb("picked_pairs", [P, J], U32, on=on)
+            nc.vector.tensor_copy(picked[2][:], b_pairs[:].rearrange("p c e -> p (c e)").bitcast(U32).indirect(second_list[:]))
+
+        def turn_pairs():
+            r_turned = bank("r_turned1", 3)
+            for t in range(PACK):
+                nc.tensor.transpose(r_turned[:, t * P : (t + 1) * P], picked[2][:].bitcast(F32)[:, t:J:PACK], ident[:])
+            nc.scalar.copy(r_woven[1][:], r_turned[:].bitcast(BF16).rearrange("p (t d e) -> p e d t", t=PACK, e=2))
+
+        def turn_rows(k):
+            r_turned = bank("r_turned%d" % k, 2 + k)
+            for e in range(2):
+                pairs = picked[2 * k + e][:].bitcast(F32)
+                for u in range(2):
+                    nc.tensor.transpose(r_turned[:, (2 * e + u) * P : (2 * e + u + 1) * P], pairs[:, u : 2 * P : 2], ident[:])
+            nc.scalar.copy(
+                r_woven[k][:].rearrange("p e d t -> p (e d t)").bitcast(F32).rearrange("p (e d u) -> p e d u", e=2, u=2),
+                r_turned[:].rearrange("p (e u d) -> p e d u", e=2, u=2),
             )
 
-        r_codes = sb("r_codes", [P, D], U32)
-        r_scales = sb("r_scales", [P, D], U8)
-        r_woven = [sb("r_woven%d" % k, [P, 2, P, PACK], BF16) for k in range(2)]
+        def quantise_rows(k, on=None):
+            r_codes[k] = sb("r_codes%d" % k, [P, 2 * P], U32, on=on)
+            r_scales[k] = sb("r_scales%d" % k, [P, 2 * P], U8)
+            nc.vector.quantize_mx(r_codes[k][:].bitcast(FP8X4), r_scales[k][:], r_woven[k][:].rearrange("p e d t -> p (e d t)"))
 
-        def pick_rows(k):
-            picked = sb("picked%d" % k, [P, J], U32)
-            nc.vector.tensor_copy(picked[:], b_pairs[k][:].rearrange("p c e -> p (c e)").bitcast(U32).indirect(second_list[:]))
-            r_turned = bank("r_turned%d" % k, 2 + k)
-            for t in range(PACK):
-                nc.tensor.transpose(r_turned[:, t * P : (t + 1) * P], picked[:].bitcast(F32)[:, t:J:PACK], ident[:])
-            nc.scalar.copy(r_woven[k][:], r_turned[:].bitcast(BF16).rearrange("p (t d e) -> p e d t", t=PACK, e=2))
-
-        def quantise_rows(k):
-            cols = slice(2 * k * P, (2 * k + 2) * P)
-            nc.vector.quantize_mx(r_codes[:, cols].bitcast(FP8X4), r_scales[:, cols], r_woven[k][:].rearrange("p e d t -> p (e d t)"))
-
-        cast_pairs(0, 0)
+        faded_plain = [sb("faded_plain0", [P, T], F32)]
+        nc.gpsimd.tensor_tensor(faded_plain[0][:], old_plain[0][:], fade_spread, ALU.mult)
+        pick_on_vector(0)
 
         neg_max = [sb("neg_max%d" % a, [P, 1], F32) for a in range(2)]
         total = sb("total", [P, 2], F32)
+        floor = [sb("floor%d" % a, [P, 1], F32) for a in range(2)]
         inv_total = sb("inv_total", [P, 2], F32)
-        probs = sb("probs", [P, 2, J], F32, on="b_raw00")
+        probs = [sb("probs%d" % a, [P, J], F32) for a in range(2)]
         scaled = [sb("scaled%d" % a, [P, J], F32) for a in range(2)]
-        group_sum = sb("group_sum", [P, 2, G], F32)
-        denom = sb("denom", [P, 2, G], F32)
+        group_sum = [sb("group_sum%d" % a, [P, G], F32) for a in range(2)]
+        denom = [sb("denom%d" % a, [P, G], F32) for a in range(2)]
+        denom_sum = [sb("denom_sum%d" % a, [P, 1], F32) for a in range(2)]
         inv_denom = sb("inv_denom", [P, 2, G], F32)
-        ds = sb("ds", [P, 2, G], F32)
         terms = [sb("terms%d" % a, [P, G], F32) for a in range(2)]
         shift = [sb("shift%d" % a, [P, 1], F32) for a in range(2)]
-        gs = [sb("gs%d" % a, [P, J], BF16) for a in range(2)]
         g_woven = [sb("g_woven%d" % a, [P, P * PACK], BF16) for a in range(2)]
-        g_codes = sb("g_codes", [P, I], U32)
-        g_scales = sb("g_scales", [P, I], U8)
+        g_codes, g_scales = {}, {}
 
         for a in range(2):
             nc.vector.tensor_reduce(neg_max[a][:], scores[a][:], AXIS_X, ALU.max, negate=True)
-            nc.scalar.activation(probs[:, a, :], scores[a][:], ACT.Exp, bias=neg_max[a][:], accum_out=total[:, a : a + 1])
-            nc.gpsimd.tensor_tensor(scaled[a][:], probs[:, a, :], js_spread, ALU.mult)
-        cast_pairs(0, 1)
-        cast_pairs(1, 0)
-        cast_pairs(1, 1)
+            nc.scalar.activation(probs[a][:], scores[a][:], ACT.Exp, bias=neg_max[a][:], accum_out=total[:, a : a + 1])
+            nc.gpsimd.tensor_tensor(scaled[a][:], probs[a][:], js_spread, ALU.mult)
+        pick_on_scalar(1)
+        turn_rows(0)
+        cast_pairs()
         for a in range(2):
-            nc.vector.tensor_reduce(group_sum[:, a, :], probs[:, a, :].rearrange("p (g r) -> p g r", r=GROUP), AXIS_X, ALU.add)
-        nc.vector.scalar_tensor_tensor(
-            denom[:], total[:].unsqueeze(2).to_broadcast([P, 2, G]), EPS, group_sum[:], ALU.mult, ALU.add
-        )
+            nc.vector.tensor_reduce(group_sum[a][:], probs[a][:].rearrange("p (g r) -> p g r", r=GROUP), AXIS_X, ALU.add)
+            nc.vector.tensor_scalar(floor[a][:], total[:, a : a + 1], EPS, None, ALU.mult)
+            nc.vector.tensor_scalar(denom[a][:], group_sum[a][:], floor[a][:], None, ALU.add, ALU.max, accum_out=denom_sum[a][:])
+            nc.vector.reciprocal(inv_denom[:, a, :], denom[a][:])
         nc.vector.reciprocal(inv_total[:], total[:])
-        nc.vector.reciprocal(inv_denom[:], denom[:])
-        pick_rows(0)
-        pick_rows(1)
+        ds = sb("ds", [P, 2, G], F32)
         nc.vector.tensor_tensor(ds[:], inv_denom[:], weights[:], ALU.mult)
         for a in range(2):
             nc.vector.scalar_tensor_tensor(
-                terms[a][:], ds[:, a, :], inv_total[:, a : a + 1], group_sum[:, a, :], ALU.mult, ALU.mult, accum_out=shift[a][:]
+                terms[a][:], ds[:, a, :], inv_total[:, a : a + 1], group_sum[a][:], ALU.mult, ALU.mult, accum_out=shift[a][:]
             )
-        for a in range(2):
+
+        def score_gradient(a, on=None):
+            gs = sb("gs%d" % a, [P, J], BF16, on=on)
             nc.vector.scalar_tensor_tensor(
-                gs[a][:].rearrange("p (g r) -> p g r", r=GROUP),
+                gs[:].rearrange("p (g r) -> p g r", r=GROUP),
                 ds[:, a, :].unsqueeze(2).to_broadcast([P, G, GROUP]),
                 shift[a][:],
                 scaled[a][:].rearrange("p (g r) -> p g r", r=GROUP),
                 ALU.subtract, ALU.mult,
             )
             g_turned = bank("g_turned%d" % a, a)
-            pairs = gs[a][:].bitcast(F32)
+            pairs = gs[:].bitcast(F32)
             for u in range(2):
                 nc.tensor.transpose(g_turned[:, u * P : (u + 1) * P], pairs[:, u : 2 * P : 2], ident[:])
             nc.scalar.copy(
@@ -197,35 +225,54 @@ def tile_attend_bgrouplogshare_x_kernel(tc, taba, tabb_words, tabb_scales, gw, j
                 g_turned[:, 0 : 2 * P].rearrange("p (u i) -> p i u", u=2),
             )
 
-        def product(into, m, cols):
-            rows = slice(m * P, (m + 1) * P)
+        def quantise_gradient(a, on=None):
+            g_codes[a] = sb("g_codes%d" % a, [P, P], U32, on=on)
+            g_scales[a] = sb("g_scales%d" % a, [P, P], U8)
+            nc.vector.quantize_mx(g_codes[a][:].bitcast(FP8X4), g_scales[a][:], g_woven[a][:])
+
+        def product(into, m, a):
+            k, e = divmod(m, 2)
+            rows = slice(e * P, (e + 1) * P)
             nc.tensor.matmul_mx(
-                into, lhsT=r_codes[:, rows].bitcast(FP8X4), lhsT_scale=r_scales[:, rows],
-                rhs=g_codes[:, cols].bitcast(FP8X4), rhs_scale=g_scales[:, cols], start=True, stop=True,
+                into, lhsT=r_codes[k][:, rows].bitcast(FP8X4), lhsT_scale=r_scales[k][:, rows],
+                rhs=g_codes[a][:].bitcast(FP8X4), rhs_scale=g_scales[a][:], start=True, stop=True,
             )
 
+        def scatter(m, a, values):
+            nc.vector.tensor_copy(windows[m][:].indirect(first_list[:, 8 * a : 8 * a + 8]), values)
+
+        score_gradient(0)
+        score_gradient(1)
+        pick_pairs(on="scaled0")
         quantise_rows(0)
-        early = [sb("early%d" % a, [P, 2, P], F32) for a in range(2)]
-        for a in range(2):
-            cols = slice(a * P, (a + 1) * P)
-            nc.vector.quantize_mx(g_codes[:, cols].bitcast(FP8X4), g_scales[:, cols], g_woven[a][:])
-            early_bank = bank("early_bank%d" % a, (2, 0)[a])
-            for m in range(2):
-                product(early_bank[:, m * P : (m + 1) * P], m, cols)
-            nc.scalar.copy(early[a][:].rearrange("p m i -> p (m i)"), early_bank[:, 0 : 2 * P])
-        faded_first = sb("faded_first", [P, T], F32, on="g_woven1")
-        nc.gpsimd.tensor_tensor(faded_first[:], old_plain[:], fade_spread, ALU.mult)
+        quantise_gradient(0)
+        first = sb("first", [P, 2, P], F32)
+        first_bank = bank("first_bank", 2)
+        for m in range(2):
+            product(first_bank[:, m * P : (m + 1) * P], m, 0)
+        nc.vector.tensor_copy(first[:].rearrange("p m i -> p (m i)"), first_bank[:, 0 : 2 * P])
+        quantise_gradient(1)
+        faded_plain.append(sb("faded_plain1", [P, T], F32, on="g_woven1"))
+        nc.gpsimd.tensor_tensor(faded_plain[1][:], old_plain[1][:], fade_spread, ALU.mult)
+        second = sb("second", [P, 2, P], F32)
+        second_bank = bank("second_bank", 0)
+        for m in range(2):
+            product(second_bank[:, m * P : (m + 1) * P], m, 1)
+        nc.scalar.copy(second[:].rearrange("p m i -> p (m i)"), second_bank[:, 0 : 2 * P])
+        for m, a in ((0, 0), (1, 0), (0, 1), (1, 1)):
+            scatter(m, a, (first, second)[a][:, m, :])
+        turn_pairs()
         quantise_rows(1)
         late = {m: sb("late%d" % m, [P, I], F32) for m in (2, 3)}
         for m in (2, 3):
             late_bank = bank("late_bank%d" % m, (1, 3)[m - 2])
-            product(late_bank[:, 0:I], m, slice(0, I))
+            for a in range(2):
+                product(late_bank[:, a * P : (a + 1) * P], m, a)
             nc.scalar.copy(late[m][:], late_bank[:, 0:I])
-
         faded = [sb("faded%d" % b, [P, turned_planes, P], F32) for b in range(8)]
         for b in range(8):
             h, bb = divmod(b, 4)
-            old_turned = bank("old_turned%d" % b, 4 + b % 4)
+            old_turned = bank("old_turned%d" % b, (2, 0, 1, 3)[b % 4])
             for n in range(turned_planes):
                 nc.tensor.transpose(old_turned[:, n * P : (n + 1) * P], old_half[h][:, n, bb * P : (bb + 1) * P], ident[:])
             nc.scalar.activation(
@@ -233,25 +280,24 @@ def tile_attend_bgrouplogshare_x_kernel(tc, taba, tabb_words, tabb_scales, gw, j
             )
 
         out_rows = out.rearrange("(m p) c -> p m c", p=P)
-        for a in range(2):
-            for m in range(2):
-                nc.vector.tensor_copy(windows[m][:].indirect(first_list[:, 8 * a : 8 * a + 8]), early[a][:, m, :])
-        for m in (2, 3):
-            nc.vector.tensor_copy(windows[m][:].indirect(first_list[:]), late[m][:])
         for n in range(8):
             m, h = divmod(n, 2)
             half = slice(h * BANK, (h + 1) * BANK)
+            if m >= 2 and h == 0:
+                nc.vector.tensor_copy(windows[m][:].indirect(first_list[:]), late[m][:])
             result = sb("result%d" % n, [P, BANK], F32)
-            if m == 0:
-                nc.gpsimd.tensor_tensor(result[:], faded_first[:, half], windows[m][:, half], ALU.add)
+            if m < 2:
+                nc.gpsimd.tensor_tensor(result[:], faded_plain[m][:, half], windows[m][:, half], ALU.add)
+                nc.sync.dma_start(out_rows[:, m, half], result[:])
+                continue
+            back = bank("back%d" % n, n)
+            for bb in range(4):
+                nc.tensor.transpose(back[:, bb * P : (bb + 1) * P], faded[4 * h + bb][:, m - 2, :], ident[:])
+            if n == -1:
+                faded_back = sb("faded_back", [P, BANK], F32)
+                nc.scalar.copy(faded_back[:], back[:])
+                nc.gpsimd.tensor_tensor(result[:], faded_back[:], windows[m][:, half], ALU.add)
+                nc.sync.dma_start(out_rows[:, m, half], result[:])
             else:
-                back = bank("back%d" % n, (4, 5, 6, 4, 5, 6)[n - 2])
-                for bb in range(4):
-                    nc.tensor.transpose(back[:, bb * P : (bb + 1) * P], faded[4 * h + bb][:, m - 1, :], ident[:])
-                if n < 4:
-                    faded_back = sb("faded_back%d" % n, [P, BANK], F32)
-                    nc.scalar.copy(faded_back[:], back[:])
-                    nc.gpsimd.tensor_tensor(result[:], faded_back[:], windows[m][:, half], ALU.add)
-                else:
-                    nc.vector.tensor_tensor(result[:], back[:], windows[m][:, half], ALU.add)
-            (nc.sync if n < 4 else nc.scalar).dma_start(out_rows[:, m, half], result[:])
+                nc.vector.tensor_tensor(result[:], back[:], windows[m][:, half], ALU.add)
+                nc.scalar.dma_start(out_rows[:, m, half], result[:])

@@ -23,6 +23,9 @@ PACK = 4
 BANK = 512
 GROUP = J // G
 EPS = 0.002
+LIST_ROWS = 16
+FADE_ROWS = T // P
+JS_ROWS = J // P
 
 
 def tile_attend_bgrouplogshare_x_kernel(tc, taba, tabb_words, tabb_scales, gw, js, brows, old, fade, offs, offs2, out):
@@ -37,9 +40,14 @@ def tile_attend_bgrouplogshare_x_kernel(tc, taba, tabb_words, tabb_scales, gw, j
         def bank(name, number):
             return psum.tile([P, BANK], F32, name=name, tag="bank%d" % number)
 
-        first_list = keep.tile([P, I // 16], U16, name="first_list")
-        second_list = keep.tile([P, J // 16], U16, name="second_list")
+        def block(n):
+            return slice(n * P, (n + 1) * P)
 
+        def half(h):
+            return slice(h * BANK, (h + 1) * BANK)
+
+        first_list = keep.tile([P, I // LIST_ROWS], U16, name="first_list")
+        second_list = keep.tile([P, J // LIST_ROWS], U16, name="second_list")
         scale_table = sb("scale_table", [P, U], U8)
         nc.gpsimd.memset(scale_table[:].bitcast(I32), 0)
         nc.sync.dma_start(second_list[:], offs2)
@@ -55,49 +63,50 @@ def tile_attend_bgrouplogshare_x_kernel(tc, taba, tabb_words, tabb_scales, gw, j
         make_identity(nc, ident[:])
         taba_rows = taba.rearrange("(p t) c -> p t c", t=PACK)
         a_first = sb("a_first", [P, 2, T], F32)
-        a_planes = [a_first[:, 0, :], a_first[:, 1, :]]
+        a_places = [a_first[:, 0, :], a_first[:, 1, :]]
         nc.sync.dma_start(a_first[:], taba_rows[:, 0:2, :])
         nc.sync.dma_start(first_list[:], offs)
-        nc.sync.dma_start(vec_rows[8:12, :], js.rearrange("o (b p) -> (o b) p", p=P))
-        nc.sync.dma_start(vec_rows[0:8, :], fade.rearrange("o (b p) -> (o b) p", p=P))
+        nc.sync.dma_start(vec_rows[FADE_ROWS : FADE_ROWS + JS_ROWS, :], js.rearrange("o (b p) -> (o b) p", p=P))
+        nc.sync.dma_start(vec_rows[0:FADE_ROWS, :], fade.rearrange("o (b p) -> (o b) p", p=P))
         for t in range(2, PACK):
-            a_plane = sb("a_plane%d" % t, [P, T], F32)
-            nc.sync.dma_start(a_plane[:], taba_rows[:, t, :])
-            a_planes.append(a_plane[:])
+            a_place = sb("a_place%d" % t, [P, T], F32)
+            nc.sync.dma_start(a_place[:], taba_rows[:, t, :])
+            a_places.append(a_place[:])
         weights = sb("weights", [P, 2, G], F32)
         nc.sync.dma_start(weights[:], gw.rearrange("(a p) g -> p a g", p=P))
 
         brows_rows = brows.rearrange("(m p) c -> p m c", p=P)
         old_rows = old.rearrange("(m p) c -> p m c", p=P)
-        old_plain = [sb("old_plain%d" % m, [P, T], F32) for m in range(2)]
+        out_rows = out.rearrange("(m p) c -> p m c", p=P)
         b_planes = [sb("b_plane%d" % m, [P, U], F32) for m in range(2)]
+        b_upper = [sb("b_upper%d" % h, [P, 2, BANK], F32) for h in range(2)]
+        old_plain = [sb("old_plain%d" % m, [P, T], F32) for m in range(2)]
+        old_upper = [sb("old_upper%d" % h, [P, 2, BANK], F32) for h in range(2)]
         nc.sync.dma_start(b_planes[0][:], brows_rows[:, 0, :])
         nc.sync.dma_start(old_plain[0][:], old_rows[:, 0, :])
         nc.sync.dma_start(b_planes[1][:], brows_rows[:, 1, :])
-        b_raw = [sb("b_raw%d" % h, [P, 2, BANK], F32) for h in range(2)]
         for h in range(2):
-            nc.sync.dma_start(b_raw[h][:], brows_rows[:, 2:4, h * BANK : (h + 1) * BANK])
-        turned_planes = 2
-        old_half = [sb("old_half%d" % h, [P, turned_planes, BANK], F32) for h in range(2)]
+            nc.sync.dma_start(b_upper[h][:], brows_rows[:, 2:4, half(h)])
         for h in range(2):
-            nc.sync.dma_start(old_half[h][:], old_rows[:, 2:4, h * BANK : (h + 1) * BANK])
+            nc.sync.dma_start(old_upper[h][:], old_rows[:, 2:4, half(h)])
         nc.sync.dma_start(old_plain[1][:], old_rows[:, 1, :])
 
         windows = [sb("window%d" % m, [P, T], F32) for m in range(4)]
-        for m in range(4):
-            (nc.vector if m < 1 else nc.gpsimd).memset(windows[m][:], 0.0)
+        nc.vector.memset(windows[0][:], 0.0)
+        for m in range(1, 4):
+            nc.gpsimd.memset(windows[m][:], 0.0)
 
         vec_turned = bank("vec_turned", 5)
         nc.tensor.transpose(vec_turned[:, 0:P], vec_rows[:], ident[:])
         vec_cols = sb("vec_cols", [P, 16], F32)
         nc.scalar.activation(vec_cols[:], vec_turned[:, 0:16], ACT.Copy)
-        spread = sb("spread", [P, 3 * BANK], F32)
-        for n in range(3):
+        spread = sb("spread", [P, T + J], F32)
+        for n in range((T + J) // BANK):
             spread_bank = bank("spread_bank%d" % n, (6, 7, 4)[n])
             for c in range(4):
                 column = vec_cols[:, 4 * n + c : 4 * n + c + 1]
-                nc.tensor.transpose(spread_bank[:, c * P : (c + 1) * P], column.to_broadcast([P, P]), ident[:])
-            nc.scalar.copy(spread[:, n * BANK : (n + 1) * BANK], spread_bank[:])
+                nc.tensor.transpose(spread_bank[:, block(c)], column.to_broadcast([P, P]), ident[:])
+            nc.scalar.copy(spread[:, half(n)], spread_bank[:])
         fade_spread = spread[:, 0:T]
         js_spread = spread[:, T : T + J]
 
@@ -107,108 +116,80 @@ def tile_attend_bgrouplogshare_x_kernel(tc, taba, tabb_words, tabb_scales, gw, j
         nc.vector.tensor_copy(b_scales[:], scale_table[:].indirect(second_list[:]))
         a_woven = sb("a_woven", [P, I, PACK], BF16)
         for t in range(PACK):
-            nc.vector.tensor_copy(a_woven[:, :, t], a_planes[t].indirect(first_list[:]))
+            nc.vector.tensor_copy(a_woven[:, :, t], a_places[t].indirect(first_list[:]))
         a_codes = sb("a_codes", [P, I], U32)
         a_scales = sb("a_scales", [P, I], U8)
         nc.vector.quantize_mx(a_codes[:].bitcast(FP8X4), a_scales[:], a_woven[:].rearrange("p i t -> p (i t)"))
-
         scores = [bank("scores%d" % a, a) for a in range(2)]
         for a in range(2):
-            cols = slice(a * P, (a + 1) * P)
             nc.tensor.matmul_mx(
-                scores[a][:], lhsT=a_codes[:, cols].bitcast(FP8X4), lhsT_scale=a_scales[:, cols],
+                scores[a][:], lhsT=a_codes[:, block(a)].bitcast(FP8X4), lhsT_scale=a_scales[:, block(a)],
                 rhs=b_words[:].bitcast(FP4X4), rhs_scale=b_scales[:], start=True, stop=True,
             )
 
-        r_codes, r_scales = {}, {}
-        r_woven = [sb("r_woven%d" % k, [P, 2, P, PACK], BF16) for k in range(2)]
-        picked = {}
-
-        def pick_on_vector(m, on=None):
-            picked[m] = sb("picked%d" % m, [P, J], BF16, on=on)
-            nc.vector.tensor_copy(picked[m][:], b_planes[m][:].indirect(second_list[:]))
-
-        def pick_on_scalar(m, on=None, on2=None):
-            rounded = sb("rounded%d" % m, [P, U], BF16, on=on)
-            nc.scalar.activation(rounded[:], b_planes[m][:], ACT.Copy)
-            picked[m] = sb("picked%d" % m, [P, J], BF16, on=on2)
-            for h in range(1):
-                n = J // 1
-                nc.scalar.activation(picked[m][:, h * n : (h + 1) * n], rounded[:].indirect(second_list[:, h * n // 16 : (h + 1) * n // 16]), ACT.Copy)
-
-        b_pairs = sb("b_pairs", [P, U, 2], BF16)
-
-        def cast_pairs():
-            for h in range(2):
-                nc.scalar.activation(b_pairs[:, h * BANK : (h + 1) * BANK, :], b_raw[h][:].rearrange("p e c -> p c e"), ACT.Copy)
-
-        def pick_pairs(on=None):
-            picked[2] = sb("picked_pairs", [P, J], U32, on=on)
-            nc.vector.tensor_copy(picked[2][:], b_pairs[:].rearrange("p c e -> p (c e)").bitcast(U32).indirect(second_list[:]))
-
-        def turn_pairs():
-            r_turned = bank("r_turned1", 3)
-            for t in range(PACK):
-                nc.tensor.transpose(r_turned[:, t * P : (t + 1) * P], picked[2][:].bitcast(F32)[:, t:J:PACK], ident[:])
-            nc.scalar.copy(r_woven[1][:], r_turned[:].bitcast(BF16).rearrange("p (t d e) -> p e d t", t=PACK, e=2))
-
-        def turn_rows(k):
-            r_turned = bank("r_turned%d" % k, 2 + k)
-            for e in range(2):
-                pairs = picked[2 * k + e][:].bitcast(F32)
+        def turn_and_weave(sources, woven, name, number):
+            turned = bank(name, number)
+            for e, values in enumerate(sources):
                 for u in range(2):
-                    nc.tensor.transpose(r_turned[:, (2 * e + u) * P : (2 * e + u + 1) * P], pairs[:, u : 2 * P : 2], ident[:])
+                    nc.tensor.transpose(turned[:, block(2 * e + u)], values.bitcast(F32)[:, u : 2 * P : 2], ident[:])
             nc.scalar.copy(
-                r_woven[k][:].rearrange("p e d t -> p (e d t)").bitcast(F32).rearrange("p (e d u) -> p e d u", e=2, u=2),
-                r_turned[:].rearrange("p (e u d) -> p e d u", e=2, u=2),
+                woven.bitcast(F32).rearrange("p (e x u) -> p e x u", x=P, u=2),
+                turned[:, 0 : len(sources) * 2 * P].rearrange("p (e u x) -> p e x u", x=P, u=2),
             )
 
-        def quantise_rows(k, on=None):
-            r_codes[k] = sb("r_codes%d" % k, [P, 2 * P], U32, on=on)
-            r_scales[k] = sb("r_scales%d" % k, [P, 2 * P], U8)
-            nc.vector.quantize_mx(r_codes[k][:].bitcast(FP8X4), r_scales[k][:], r_woven[k][:].rearrange("p e d t -> p (e d t)"))
+        def quantise(name, woven, width):
+            codes = sb(name + "_codes", [P, width], U32)
+            scales = sb(name + "_scales", [P, width], U8)
+            nc.vector.quantize_mx(codes[:].bitcast(FP8X4), scales[:], woven)
+            return codes, scales
 
         faded_plain = [sb("faded_plain0", [P, T], F32)]
         nc.gpsimd.tensor_tensor(faded_plain[0][:], old_plain[0][:], fade_spread, ALU.mult)
-        pick_on_vector(0)
+        picked = [sb("picked%d" % m, [P, J], BF16) for m in range(2)]
+        nc.vector.tensor_copy(picked[0][:], b_planes[0][:].indirect(second_list[:]))
 
         neg_max = [sb("neg_max%d" % a, [P, 1], F32) for a in range(2)]
         total = sb("total", [P, 2], F32)
-        floor = [sb("floor%d" % a, [P, 1], F32) for a in range(2)]
-        inv_total = sb("inv_total", [P, 2], F32)
         probs = [sb("probs%d" % a, [P, J], F32) for a in range(2)]
         scaled = [sb("scaled%d" % a, [P, J], F32) for a in range(2)]
-        group_sum = [sb("group_sum%d" % a, [P, G], F32) for a in range(2)]
-        denom = [sb("denom%d" % a, [P, G], F32) for a in range(2)]
-        denom_sum = [sb("denom_sum%d" % a, [P, 1], F32) for a in range(2)]
-        inv_denom = sb("inv_denom", [P, 2, G], F32)
-        terms = [sb("terms%d" % a, [P, G], F32) for a in range(2)]
-        shift = [sb("shift%d" % a, [P, 1], F32) for a in range(2)]
-        g_woven = [sb("g_woven%d" % a, [P, P * PACK], BF16) for a in range(2)]
-        g_codes, g_scales = {}, {}
-
         for a in range(2):
             nc.vector.tensor_reduce(neg_max[a][:], scores[a][:], AXIS_X, ALU.max, negate=True)
             nc.scalar.activation(probs[a][:], scores[a][:], ACT.Exp, bias=neg_max[a][:], accum_out=total[:, a : a + 1])
             nc.gpsimd.tensor_tensor(scaled[a][:], probs[a][:], js_spread, ALU.mult)
-        pick_on_scalar(1)
-        turn_rows(0)
-        cast_pairs()
+
+        rounded = sb("rounded", [P, U], BF16)
+        nc.scalar.activation(rounded[:], b_planes[1][:], ACT.Copy)
+        nc.scalar.activation(picked[1][:], rounded[:].indirect(second_list[:]), ACT.Copy)
+        lower_woven = sb("lower_woven", [P, 2 * P * PACK], BF16)
+        turn_and_weave([picked[0][:], picked[1][:]], lower_woven[:], "lower_turned", 2)
+        b_pairs = sb("b_pairs", [P, U, 2], BF16)
+        for h in range(2):
+            nc.scalar.activation(b_pairs[:, half(h), :], b_upper[h][:].rearrange("p e c -> p c e"), ACT.Copy)
+
+        group_sum = [sb("group_sum%d" % a, [P, G], F32) for a in range(2)]
+        inv_denom = sb("inv_denom", [P, 2, G], F32)
         for a in range(2):
             nc.vector.tensor_reduce(group_sum[a][:], probs[a][:].rearrange("p (g r) -> p g r", r=GROUP), AXIS_X, ALU.add)
-            nc.vector.tensor_scalar(floor[a][:], total[:, a : a + 1], EPS, None, ALU.mult)
-            nc.vector.tensor_scalar(denom[a][:], group_sum[a][:], floor[a][:], None, ALU.add, ALU.max, accum_out=denom_sum[a][:])
-            nc.vector.reciprocal(inv_denom[:, a, :], denom[a][:])
+            floor = sb("floor%d" % a, [P, 1], F32)
+            nc.vector.tensor_scalar(floor[:], total[:, a : a + 1], EPS, None, ALU.mult)
+            denom = sb("denom%d" % a, [P, G], F32)
+            denom_max = sb("denom_max%d" % a, [P, 1], F32)
+            nc.vector.tensor_scalar(denom[:], group_sum[a][:], floor[:], None, ALU.add, ALU.max, accum_out=denom_max[:])
+            nc.vector.reciprocal(inv_denom[:, a, :], denom[:])
+        inv_total = sb("inv_total", [P, 2], F32)
         nc.vector.reciprocal(inv_total[:], total[:])
         ds = sb("ds", [P, 2, G], F32)
         nc.vector.tensor_tensor(ds[:], inv_denom[:], weights[:], ALU.mult)
+        shift = [sb("shift%d" % a, [P, 1], F32) for a in range(2)]
         for a in range(2):
+            terms = sb("terms%d" % a, [P, G], F32)
             nc.vector.scalar_tensor_tensor(
-                terms[a][:], ds[:, a, :], inv_total[:, a : a + 1], group_sum[a][:], ALU.mult, ALU.mult, accum_out=shift[a][:]
+                terms[:], ds[:, a, :], inv_total[:, a : a + 1], group_sum[a][:], ALU.mult, ALU.mult, accum_out=shift[a][:]
             )
 
-        def score_gradient(a, on=None):
-            gs = sb("gs%d" % a, [P, J], BF16, on=on)
+        g_woven = [sb("g_woven%d" % a, [P, P * PACK], BF16) for a in range(2)]
+        for a in range(2):
+            gs = sb("gs%d" % a, [P, J], BF16)
             nc.vector.scalar_tensor_tensor(
                 gs[:].rearrange("p (g r) -> p g r", r=GROUP),
                 ds[:, a, :].unsqueeze(2).to_broadcast([P, G, GROUP]),
@@ -216,88 +197,79 @@ def tile_attend_bgrouplogshare_x_kernel(tc, taba, tabb_words, tabb_scales, gw, j
                 scaled[a][:].rearrange("p (g r) -> p g r", r=GROUP),
                 ALU.subtract, ALU.mult,
             )
-            g_turned = bank("g_turned%d" % a, a)
-            pairs = gs[:].bitcast(F32)
-            for u in range(2):
-                nc.tensor.transpose(g_turned[:, u * P : (u + 1) * P], pairs[:, u : 2 * P : 2], ident[:])
-            nc.scalar.copy(
-                g_woven[a][:].bitcast(F32).rearrange("p (i u) -> p i u", u=2),
-                g_turned[:, 0 : 2 * P].rearrange("p (u i) -> p i u", u=2),
-            )
+            turn_and_weave([gs[:]], g_woven[a][:], "g_turned%d" % a, a)
 
-        def quantise_gradient(a, on=None):
-            g_codes[a] = sb("g_codes%d" % a, [P, P], U32, on=on)
-            g_scales[a] = sb("g_scales%d" % a, [P, P], U8)
-            nc.vector.quantize_mx(g_codes[a][:].bitcast(FP8X4), g_scales[a][:], g_woven[a][:])
+        picked_pairs = sb("picked_pairs", [P, J], U32, on="scaled0")
+        nc.vector.tensor_copy(picked_pairs[:], b_pairs[:].rearrange("p c e -> p (c e)").bitcast(U32).indirect(second_list[:]))
+        rows = {0: quantise("lower", lower_woven[:], 2 * P)}
 
         def product(into, m, a):
-            k, e = divmod(m, 2)
-            rows = slice(e * P, (e + 1) * P)
+            (r_codes, r_scales), (g_codes, g_scales) = rows[m // 2], grads[a]
+            cols = block(m % 2)
             nc.tensor.matmul_mx(
-                into, lhsT=r_codes[k][:, rows].bitcast(FP8X4), lhsT_scale=r_scales[k][:, rows],
-                rhs=g_codes[a][:].bitcast(FP8X4), rhs_scale=g_scales[a][:], start=True, stop=True,
+                into, lhsT=r_codes[:, cols].bitcast(FP8X4), lhsT_scale=r_scales[:, cols],
+                rhs=g_codes[:].bitcast(FP8X4), rhs_scale=g_scales[:], start=True, stop=True,
             )
 
-        def scatter(m, a, values):
-            nc.vector.tensor_copy(windows[m][:].indirect(first_list[:, 8 * a : 8 * a + 8]), values)
+        def scatter(m, entries, values):
+            nc.vector.tensor_copy(windows[m][:].indirect(first_list[:, entries.start // LIST_ROWS : entries.stop // LIST_ROWS]), values)
 
-        score_gradient(0)
-        score_gradient(1)
-        pick_pairs(on="scaled0")
-        quantise_rows(0)
-        quantise_gradient(0)
-        first = sb("first", [P, 2, P], F32)
+        grads = {0: quantise("g0", g_woven[0][:], P)}
+        first = sb("first", [P, P], F32)
         first_bank = bank("first_bank", 2)
-        for m in range(2):
-            product(first_bank[:, m * P : (m + 1) * P], m, 0)
-        nc.vector.tensor_copy(first[:].rearrange("p m i -> p (m i)"), first_bank[:, 0 : 2 * P])
-        quantise_gradient(1)
+        product(first_bank[:, 0:P], 0, 0)
+        nc.vector.tensor_copy(first[:], first_bank[:, 0:P])
+        grads[1] = quantise("g1", g_woven[1][:], P)
         faded_plain.append(sb("faded_plain1", [P, T], F32, on="g_woven1"))
         nc.gpsimd.tensor_tensor(faded_plain[1][:], old_plain[1][:], fade_spread, ALU.mult)
-        second = sb("second", [P, 2, P], F32)
+        second = sb("second", [P, 3 * P], F32)
         second_bank = bank("second_bank", 0)
-        for m in range(2):
-            product(second_bank[:, m * P : (m + 1) * P], m, 1)
-        nc.scalar.copy(second[:].rearrange("p m i -> p (m i)"), second_bank[:, 0 : 2 * P])
-        for m, a in ((0, 0), (1, 0), (0, 1), (1, 1)):
-            scatter(m, a, (first, second)[a][:, m, :])
-        turn_pairs()
-        quantise_rows(1)
-        late = {m: sb("late%d" % m, [P, I], F32) for m in (2, 3)}
-        for m in (2, 3):
-            late_bank = bank("late_bank%d" % m, (1, 3)[m - 2])
-            for a in range(2):
-                product(late_bank[:, a * P : (a + 1) * P], m, a)
-            nc.scalar.copy(late[m][:], late_bank[:, 0:I])
-        faded = [sb("faded%d" % b, [P, turned_planes, P], F32) for b in range(8)]
-        for b in range(8):
-            h, bb = divmod(b, 4)
-            old_turned = bank("old_turned%d" % b, (2, 0, 1, 3)[b % 4])
-            for n in range(turned_planes):
-                nc.tensor.transpose(old_turned[:, n * P : (n + 1) * P], old_half[h][:, n, bb * P : (bb + 1) * P], ident[:])
-            nc.scalar.activation(
-                faded[b][:].rearrange("p m d -> p (m d)"), old_turned[:, 0 : turned_planes * P], ACT.Copy, scale=vec_cols[:, b : b + 1]
-            )
+        for n, (m, a) in enumerate(((0, 1), (1, 0), (1, 1))):
+            product(second_bank[:, block(n)], m, a)
+        nc.scalar.copy(second[:], second_bank[:, 0 : 3 * P])
+        scatter(0, block(0), first[:])
 
-        out_rows = out.rearrange("(m p) c -> p m c", p=P)
+        pairs_turned = bank("pairs_turned", 3)
+        for t in range(PACK):
+            nc.tensor.transpose(pairs_turned[:, block(t)], picked_pairs[:].bitcast(F32)[:, t:J:PACK], ident[:])
+        upper_woven = sb("upper_woven", [P, 2, P, PACK], BF16)
+        nc.scalar.copy(upper_woven[:], pairs_turned[:].bitcast(BF16).rearrange("p (t d e) -> p e d t", t=PACK, e=2))
+        rows[1] = quantise("upper", upper_woven[:].rearrange("p e d t -> p (e d t)"), 2 * P)
+        scatter(0, block(1), second[:, 0:P])
+        scatter(1, slice(0, I), second[:, P : 3 * P])
+
+        def whole_plane(m, number):
+            values = sb("plane_grad%d" % m, [P, I], F32)
+            into = bank("plane_bank%d" % m, number)
+            for a in range(2):
+                product(into[:, block(a)], m, a)
+            nc.scalar.copy(values[:], into[:, 0:I])
+            return values
+
+        plane_grads = {2: whole_plane(2, 1)}
+
+        faded = [sb("faded%d" % b, [P, 2, P], F32) for b in range(FADE_ROWS)]
+        for b in range(FADE_ROWS):
+            h, c = divmod(b, 4)
+            old_turned = bank("old_turned%d" % b, (2, 0, 1)[b % 3])
+            for e in range(2):
+                nc.tensor.transpose(old_turned[:, block(e)], old_upper[h][:, e, block(c)], ident[:])
+            nc.scalar.activation(
+                faded[b][:].rearrange("p e d -> p (e d)"), old_turned[:, 0 : 2 * P], ACT.Copy, scale=vec_cols[:, b : b + 1]
+            )
+        plane_grads[3] = whole_plane(3, 2)
+
         for n in range(8):
             m, h = divmod(n, 2)
-            half = slice(h * BANK, (h + 1) * BANK)
-            if m >= 2 and h == 0:
-                nc.vector.tensor_copy(windows[m][:].indirect(first_list[:]), late[m][:])
             result = sb("result%d" % n, [P, BANK], F32)
             if m < 2:
-                nc.gpsimd.tensor_tensor(result[:], faded_plain[m][:, half], windows[m][:, half], ALU.add)
-                nc.sync.dma_start(out_rows[:, m, half], result[:])
-                continue
-            back = bank("back%d" % n, n)
-            for bb in range(4):
-                nc.tensor.transpose(back[:, bb * P : (bb + 1) * P], faded[4 * h + bb][:, m - 2, :], ident[:])
-            if n == -1:
-                faded_back = sb("faded_back", [P, BANK], F32)
-                nc.scalar.copy(faded_back[:], back[:])
-                nc.gpsimd.tensor_tensor(result[:], faded_back[:], windows[m][:, half], ALU.add)
-                nc.sync.dma_start(out_rows[:, m, half], result[:])
+                nc.gpsimd.tensor_tensor(result[:], faded_plain[m][:, half(h)], windows[m][:, half(h)], ALU.add)
+                nc.sync.dma_start(out_rows[:, m, half(h)], result[:])
             else:
-                nc.vector.tensor_tensor(result[:], back[:], windows[m][:, half], ALU.add)
-                nc.scalar.dma_start(out_rows[:, m, half], result[:])
+                if h == 0:
+                    scatter(m, slice(0, I), plane_grads[m][:])
+                back = bank("back%d" % n, n)
+                for c in range(4):
+                    nc.tensor.transpose(back[:, block(c)], faded[4 * h + c][:, m - 2, :], ident[:])
+                nc.vector.tensor_tensor(result[:], back[:], windows[m][:, half(h)], ALU.add)
+                nc.scalar.dma_start(out_rows[:, m, half(h)], result[:])

@@ -87,9 +87,9 @@ def tile_attend_bgrouplogshare_x_kernel(tc, taba, tabb_words, tabb_scales, gw, j
         nc.sync.dma_start(b_planes[1][:], brows_rows[:, 1, :])
         for h in range(2):
             nc.sync.dma_start(b_upper[h][:], brows_rows[:, 2:4, half(h)])
+        nc.sync.dma_start(old_plain[1][:], old_rows[:, 1, :])
         for h in range(2):
             nc.sync.dma_start(old_upper[h][:], old_rows[:, 2:4, half(h)])
-        nc.sync.dma_start(old_plain[1][:], old_rows[:, 1, :])
 
         windows = [sb("window%d" % m, [P, T], F32) for m in range(4)]
         nc.vector.memset(windows[0][:], 0.0)
@@ -143,8 +143,9 @@ def tile_attend_bgrouplogshare_x_kernel(tc, taba, tabb_words, tabb_scales, gw, j
             nc.vector.quantize_mx(codes[:].bitcast(FP8X4), scales[:], woven)
             return codes, scales
 
-        faded_plain = [sb("faded_plain0", [P, T], F32)]
-        nc.gpsimd.tensor_tensor(faded_plain[0][:], old_plain[0][:], fade_spread, ALU.mult)
+        faded_plane0 = sb("faded_plane0", [P, T], F32)
+        nc.gpsimd.tensor_tensor(faded_plane0[:], old_plain[0][:], fade_spread, ALU.mult)
+        faded_lower = [faded_plane0[:, half(h)] for h in range(2)]
         picked = [sb("picked%d" % m, [P, J], BF16) for m in range(2)]
         nc.vector.tensor_copy(picked[0][:], b_planes[0][:].indirect(second_list[:]))
 
@@ -199,6 +200,12 @@ def tile_attend_bgrouplogshare_x_kernel(tc, taba, tabb_words, tabb_scales, gw, j
             )
             turn_and_weave([gs[:]], g_woven[a][:], "g_turned%d" % a, a)
 
+        def fade_half_of_plane1(h, on):
+            values = sb("faded_plane1_%d" % h, [P, BANK], F32, on=on)
+            nc.gpsimd.tensor_tensor(values[:], old_plain[1][:, half(h)], fade_spread[:, half(h)], ALU.mult)
+            faded_lower.append(values[:])
+
+        fade_half_of_plane1(0, "scaled1")
         picked_pairs = sb("picked_pairs", [P, J], U32, on="scaled0")
         nc.vector.tensor_copy(picked_pairs[:], b_pairs[:].rearrange("p c e -> p (c e)").bitcast(U32).indirect(second_list[:]))
         rows = {0: quantise("lower", lower_woven[:], 2 * P)}
@@ -220,8 +227,7 @@ def tile_attend_bgrouplogshare_x_kernel(tc, taba, tabb_words, tabb_scales, gw, j
         product(first_bank[:, 0:P], 0, 0)
         nc.vector.tensor_copy(first[:], first_bank[:, 0:P])
         grads[1] = quantise("g1", g_woven[1][:], P)
-        faded_plain.append(sb("faded_plain1", [P, T], F32, on="g_woven1"))
-        nc.gpsimd.tensor_tensor(faded_plain[1][:], old_plain[1][:], fade_spread, ALU.mult)
+        fade_half_of_plane1(1, "g_woven1")
         second = sb("second", [P, 3 * P], F32)
         second_bank = bank("second_bank", 0)
         for n, (m, a) in enumerate(((0, 1), (1, 0), (1, 1))):
@@ -263,7 +269,7 @@ def tile_attend_bgrouplogshare_x_kernel(tc, taba, tabb_words, tabb_scales, gw, j
             m, h = divmod(n, 2)
             result = sb("result%d" % n, [P, BANK], F32)
             if m < 2:
-                nc.gpsimd.tensor_tensor(result[:], faded_plain[m][:, half(h)], windows[m][:, half(h)], ALU.add)
+                nc.gpsimd.tensor_tensor(result[:], faded_lower[n], windows[m][:, half(h)], ALU.add)
                 nc.sync.dma_start(out_rows[:, m, half(h)], result[:])
             else:
                 if h == 0:

from contextlib import ExitStack

import concourse.mybir as mybir
from concourse.masks import make_identity

D, T, U, I, J, G = 512, 1024, 1024, 256, 512, 64
FLOPS = 2 * D * I * J + 2 * J * D * I

F32 = mybir.dt.float32
BF16 = mybir.dt.bfloat16
I32 = mybir.dt.int32
U32 = mybir.dt.uint32
U16 = mybir.dt.uint16
U8 = mybir.dt.uint8
FP8X4 = mybir.dt.float8_e4m3fn_x4
FP4X4 = mybir.dt.float4_e2m1fn_x4
ALU = mybir.AluOpType
ACT = mybir.ActivationFunctionType
AXIS_X = mybir.AxisListType.X

P = 128
PACK = 4
BANK = 512
GROUP = J // G
EPS = 0.002
LIST_ROWS = 16
FADE_ROWS = T // P
JS_ROWS = J // P


def tile_attend_bgrouplogshare_x_kernel(tc, taba, tabb_words, tabb_scales, gw, js, brows, old, fade, offs, offs2, out):
    nc = tc.nc
    with ExitStack() as ctx:
        keep = ctx.enter_context(tc.tile_pool(name="keep", bufs=1))
        psum = ctx.enter_context(tc.psum_pool(name="psum", bufs=1))

        def sb(name, shape, dtype, on=None):
            return keep.tile(shape, dtype, name=name, tag=on or name, align_bytes=64)

        def bank(name, number):
            return psum.tile([P, BANK], F32, name=name, tag="bank%d" % number)

        def block(n):
            return slice(n * P, (n + 1) * P)

        def half(h):
            return slice(h * BANK, (h + 1) * BANK)

        first_list = keep.tile([P, I // LIST_ROWS], U16, name="first_list")
        second_list = keep.tile([P, J // LIST_ROWS], U16, name="second_list")
        scale_table = sb("scale_table", [P, U], U8)
        nc.gpsimd.memset(scale_table[:].bitcast(I32), 0)
        nc.sync.dma_start(second_list[:], offs2)
        word_table = sb("word_table", [P, U], U16)
        nc.sync.dma_start(word_table[:].bitcast(I32), tabb_words[0].bitcast(I32))
        for q in range(4):
            nc.sync.dma_start(
                scale_table[32 * q : 32 * q + 4, :].bitcast(I32), tabb_scales[0, 4 * q : 4 * q + 4, :].bitcast(I32)
            )
        ident = sb("ident", [P, P], F32)
        vec_rows = sb("vec_rows", [P, P], F32)
        nc.gpsimd.memset(vec_rows[:], 0.0)
        make_identity(nc, ident[:])
        taba_rows = taba.rearrange("(p t) c -> p t c", t=PACK)
        a_first = sb("a_first", [P, 2, T], F32)
        a_places = [a_first[:, 0, :], a_first[:, 1, :]]
        nc.sync.dma_start(a_first[:], taba_rows[:, 0:2, :])
        nc.sync.dma_start(first_list[:], offs)
        nc.sync.dma_start(vec_rows[FADE_ROWS : FADE_ROWS + JS_ROWS, :], js.rearrange("o (b p) -> (o b) p", p=P))
        nc.sync.dma_start(vec_rows[0:FADE_ROWS, :], fade.rearrange("o (b p) -> (o b) p", p=P))
        for t in range(2, PACK):
            a_place = sb("a_place%d" % t, [P, T], F32)
            nc.sync.dma_start(a_place[:], taba_rows[:, t, :])
            a_places.append(a_place[:])
        weights = sb("weights", [P, 2, G], F32)
        nc.sync.dma_start(weights[:], gw.rearrange("(a p) g -> p a g", p=P))

        brows_rows = brows.rearrange("(m p) c -> p m c", p=P)
        old_rows = old.rearrange("(m p) c -> p m c", p=P)
        out_rows = out.rearrange("(m p) c -> p m c", p=P)
        b_planes = [sb("b_plane%d" % m, [P, U], F32) for m in range(2)]
        b_upper = [sb("b_upper%d" % h, [P, 2, BANK], F32) for h in range(2)]
        old_plain = [sb("old_plain%d" % m, [P, T], F32) for m in range(2)]
        old_upper = [sb("old_upper%d" % h, [P, 2, BANK], F32) for h in range(2)]
        nc.sync.dma_start(b_planes[0][:], brows_rows[:, 0, :])
        nc.sync.dma_start(old_plain[0][:], old_rows[:, 0, :])
        nc.sync.dma_start(b_planes[1][:], brows_rows[:, 1, :])
        for h in range(2):
            nc.sync.dma_start(b_upper[h][:], brows_rows[:, 2:4, half(h)])
        nc.sync.dma_start(old_plain[1][:], old_rows[:, 1, :])
        for h in range(2):
            nc.sync.dma_start(old_upper[h][:], old_rows[:, 2:4, half(h)])

        windows = [sb("window%d" % m, [P, T], F32) for m in range(4)]
        nc.vector.memset(windows[0][:], 0.0)
        for m in range(1, 4):
            nc.gpsimd.memset(windows[m][:], 0.0)

        vec_turned = bank("vec_turned", 5)
        nc.tensor.transpose(vec_turned[:, 0:P], vec_rows[:], ident[:])
        vec_cols = sb("vec_cols", [P, 16], F32)
        nc.scalar.activation(vec_cols[:], vec_turned[:, 0:16], ACT.Copy)
        spread = sb("spread", [P, T + J], F32)
        for n in range((T + J) // BANK):
            spread_bank = bank("spread_bank%d" % n, (6, 7, 4)[n])
            for c in range(4):
                column = vec_cols[:, 4 * n + c : 4 * n + c + 1]
                nc.tensor.transpose(spread_bank[:, block(c)], column.to_broadcast([P, P]), ident[:])
            nc.scalar.copy(spread[:, half(n)], spread_bank[:])
        fade_spread = spread[:, 0:T]
        js_spread = spread[:, T : T + J]

        b_words = sb("b_words", [P, J], U16)
        nc.vector.tensor_copy(b_words[:], word_table[:].indirect(second_list[:]))
        b_scales = sb("b_scales", [P, J], U8)
        nc.vector.tensor_copy(b_scales[:], scale_table[:].indirect(second_list[:]))
        a_woven = sb("a_woven", [P, I, PACK], BF16)
        for t in range(PACK):
            nc.vector.tensor_copy(a_woven[:, :, t], a_places[t].indirect(first_list[:]))
        a_codes = sb("a_codes", [P, I], U32)
        a_scales = sb("a_scales", [P, I], U8)
        nc.vector.quantize_mx(a_codes[:].bitcast(FP8X4), a_scales[:], a_woven[:].rearrange("p i t -> p (i t)"))
        scores = [bank("scores%d" % a, a) for a in range(2)]
        for a in range(2):
            nc.tensor.matmul_mx(
                scores[a][:], lhsT=a_codes[:, block(a)].bitcast(FP8X4), lhsT_scale=a_scales[:, block(a)],
                rhs=b_words[:].bitcast(FP4X4), rhs_scale=b_scales[:], start=True, stop=True,
            )

        def turn_and_weave(sources, woven, name, number):
            turned = bank(name, number)
            for e, values in enumerate(sources):
                for u in range(2):
                    nc.tensor.transpose(turned[:, block(2 * e + u)], values.bitcast(F32)[:, u : 2 * P : 2], ident[:])
            nc.scalar.copy(
                woven.bitcast(F32).rearrange("p (e x u) -> p e x u", x=P, u=2),
                turned[:, 0 : len(sources) * 2 * P].rearrange("p (e u x) -> p e x u", x=P, u=2),
            )

        def quantise(name, woven, width):
            codes = sb(name + "_codes", [P, width], U32)
            scales = sb(name + "_scales", [P, width], U8)
            nc.vector.quantize_mx(codes[:].bitcast(FP8X4), scales[:], woven)
            return codes, scales

        faded_plane0 = sb("faded_plane0", [P, T], F32)
        nc.gpsimd.tensor_tensor(faded_plane0[:], old_plain[0][:], fade_spread, ALU.mult)
        faded_lower = [faded_plane0[:, half(h)] for h in range(2)]
        picked = [sb("picked%d" % m, [P, J], BF16) for m in range(2)]
        nc.vector.tensor_copy(picked[0][:], b_planes[0][:].indirect(second_list[:]))

        neg_max = [sb("neg_max%d" % a, [P, 1], F32) for a in range(2)]
        total = sb("total", [P, 2], F32)
        probs = [sb("probs%d" % a, [P, J], F32) for a in range(2)]
        scaled = [sb("scaled%d" % a, [P, J], F32) for a in range(2)]
        for a in range(2):
            nc.vector.tensor_reduce(neg_max[a][:], scores[a][:], AXIS_X, ALU.max, negate=True)
            nc.scalar.activation(probs[a][:], scores[a][:], ACT.Exp, bias=neg_max[a][:], accum_out=total[:, a : a + 1])
            nc.gpsimd.tensor_tensor(scaled[a][:], probs[a][:], js_spread, ALU.mult)

        rounded = sb("rounded", [P, U], BF16)
        nc.scalar.activation(rounded[:], b_planes[1][:], ACT.Copy)
        nc.scalar.activation(picked[1][:], rounded[:].indirect(second_list[:]), ACT.Copy)
        lower_woven = sb("lower_woven", [P, 2 * P * PACK], BF16)
        turn_and_weave([picked[0][:], picked[1][:]], lower_woven[:], "lower_turned", 2)
        b_pairs = sb("b_pairs", [P, U, 2], BF16)
        for h in range(2):
            nc.scalar.activation(b_pairs[:, half(h), :], b_upper[h][:].rearrange("p e c -> p c e"), ACT.Copy)

        group_sum = [sb("group_sum%d" % a, [P, G], F32) for a in range(2)]
        inv_denom = sb("inv_denom", [P, 2, G], F32)
        for a in range(2):
            nc.vector.tensor_reduce(group_sum[a][:], probs[a][:].rearrange("p (g r) -> p g r", r=GROUP), AXIS_X, ALU.add)
            floor = sb("floor%d" % a, [P, 1], F32)
            nc.vector.tensor_scalar(floor[:], total[:, a : a + 1], EPS, None, ALU.mult)
            denom = sb("denom%d" % a, [P, G], F32)
            denom_max = sb("denom_max%d" % a, [P, 1], F32)
            nc.vector.tensor_scalar(denom[:], group_sum[a][:], floor[:], None, ALU.add, ALU.max, accum_out=denom_max[:])
            nc.vector.reciprocal(inv_denom[:, a, :], denom[:])
        inv_total = sb("inv_total", [P, 2], F32)
        nc.vector.reciprocal(inv_total[:], total[:])
        ds = sb("ds", [P, 2, G], F32)
        nc.vector.tensor_tensor(ds[:], inv_denom[:], weights[:], ALU.mult)
        shift = [sb("shift%d" % a, [P, 1], F32) for a in range(2)]
        for a in range(2):
            terms = sb("terms%d" % a, [P, G], F32)
            nc.vector.scalar_tensor_tensor(
                terms[:], ds[:, a, :], inv_total[:, a : a + 1], group_sum[a][:], ALU.mult, ALU.mult, accum_out=shift[a][:]
            )

        g_woven = [sb("g_woven%d" % a, [P, P * PACK], BF16) for a in range(2)]
        for a in range(2):
            gs = sb("gs%d" % a, [P, J], BF16)
            nc.vector.scalar_tensor_tensor(
                gs[:].rearrange("p (g r) -> p g r", r=GROUP),
                ds[:, a, :].unsqueeze(2).to_broadcast([P, G, GROUP]),
                shift[a][:],
                scaled[a][:].rearrange("p (g r) -> p g r", r=GROUP),
                ALU.subtract, ALU.mult,
            )
            turn_and_weave([gs[:]], g_woven[a][:], "g_turned%d" % a, a)

        def fade_half_of_plane1(h, on):
            values = sb("faded_plane1_%d" % h, [P, BANK], F32, on=on)
            nc.gpsimd.tensor_tensor(values[:], old_plain[1][:, half(h)], fade_spread[:, half(h)], ALU.mult)
            faded_lower.append(values[:])

        fade_half_of_plane1(0, "scaled1")
        picked_pairs = sb("picked_pairs", [P, J], U32, on="scaled0")
        nc.vector.tensor_copy(picked_pairs[:], b_pairs[:].rearrange("p c e -> p (c e)").bitcast(U32).indirect(second_list[:]))
        rows = {0: quantise("lower", lower_woven[:], 2 * P)}

        def product(into, m, a):
            (r_codes, r_scales), (g_codes, g_scales) = rows[m // 2], grads[a]
            cols = block(m % 2)
            nc.tensor.matmul_mx(
                into, lhsT=r_codes[:, cols].bitcast(FP8X4), lhsT_scale=r_scales[:, cols],
                rhs=g_codes[:].bitcast(FP8X4), rhs_scale=g_scales[:], start=True, stop=True,
            )

        def scatter(m, entries, values):
            nc.vector.tensor_copy(windows[m][:].indirect(first_list[:, entries.start // LIST_ROWS : entries.stop // LIST_ROWS]), values)

        grads = {0: quantise("g0", g_woven[0][:], P)}
        first = sb("first", [P, P], F32)
        first_bank = bank("first_bank", 2)
        product(first_bank[:, 0:P], 0, 0)
        nc.vector.tensor_copy(first[:], first_bank[:, 0:P])
        grads[1] = quantise("g1", g_woven[1][:], P)
        fade_half_of_plane1(1, "g_woven1")
        second = sb("second", [P, 3 * P], F32)
        second_bank = bank("second_bank", 0)
        for n, (m, a) in enumerate(((0, 1), (1, 0), (1, 1))):
            product(second_bank[:, block(n)], m, a)
        nc.scalar.copy(second[:], second_bank[:, 0 : 3 * P])
        scatter(0, block(0), first[:])

        pairs_turned = bank("pairs_turned", 3)
        for t in range(PACK):
            nc.tensor.transpose(pairs_turned[:, block(t)], picked_pairs[:].bitcast(F32)[:, t:J:PACK], ident[:])
        upper_woven = sb("upper_woven", [P, 2, P, PACK], BF16)
        nc.scalar.copy(upper_woven[:], pairs_turned[:].bitcast(BF16).rearrange("p (t d e) -> p e d t", t=PACK, e=2))
        rows[1] = quantise("upper", upper_woven[:].rearrange("p e d t -> p (e d t)"), 2 * P)
        scatter(0, block(1), second[:, 0:P])
        scatter(1, slice(0, I), second[:, P : 3 * P])

        def whole_plane(m, number):
            values = sb("plane_grad%d" % m, [P, I], F32)
            into = bank("plane_bank%d" % m, number)
            for a in range(2):
                product(into[:, block(a)], m, a)
            nc.scalar.copy(values[:], into[:, 0:I])
            return values

        plane_grads = {2: whole_plane(2, 1)}

        faded = [sb("faded%d" % b, [P, 2, P], F32) for b in range(FADE_ROWS)]
        for b in range(FADE_ROWS):
            h, c = divmod(b, 4)
            old_turned = bank("old_turned%d" % b, (2, 0, 1)[b % 3])
            for e in range(2):
                nc.tensor.transpose(old_turned[:, block(e)], old_upper[h][:, e, block(c)], ident[:])
            nc.scalar.activation(
                faded[b][:].rearrange("p e d -> p (e d)"), old_turned[:, 0 : 2 * P], ACT.Copy, scale=vec_cols[:, b : b + 1]
            )
        plane_grads[3] = whole_plane(3, 2)

        for n in range(8):
            m, h = divmod(n, 2)
            result = sb("result%d" % n, [P, BANK], F32)
            if m < 2:
                nc.gpsimd.tensor_tensor(result[:], faded_lower[n], windows[m][:, half(h)], ALU.add)
                nc.sync.dma_start(out_rows[:, m, half(h)], result[:])
            else:
                if h == 0:
                    scatter(m, slice(0, I), plane_grads[m][:])
                back = bank("back%d" % n, n)
                for c in range(4):
                    nc.tensor.transpose(back[:, block(c)], faded[4 * h + c][:, m - 2, :], ident[:])
                nc.vector.tensor_tensor(result[:], back[:], windows[m][:, half(h)], ALU.add)
                nc.scalar.dma_start(out_rows[:, m, half(h)], result[:])
